import numpy as np
import ml_dtypes


def mxq(x, axis, fmt="e4m3"):
    dtype, down = {"e4m3": (ml_dtypes.float8_e4m3fn, 7), "e5m2": (ml_dtypes.float8_e5m2, 14)}[fmt]
    v = np.moveaxis(np.asarray(x, np.float32).astype(ml_dtypes.bfloat16).astype(np.float64), axis, -1)
    blocks = v.reshape(v.shape[:-1] + (-1, 32))
    amax = np.abs(blocks).max(-1, keepdims=True)
    byte = np.maximum(np.where(amax > 0, np.frexp(amax)[1] - 1 + 127, 0) - down, 1)
    scale = np.exp2(byte - 127.0)
    codes = (blocks / scale).astype(np.float32).astype(dtype).astype(np.float64)
    return np.moveaxis((codes * scale).reshape(v.shape), -1, axis)


WIDE = False


def mx_kscale(k):
    if not WIDE:
        return np.ones(k)
    levels = np.array([10, -10, 5, -5, 0])
    if k % 512:
        return np.exp2(np.random.permutation(np.resize(levels, k // 32))).repeat(32)
    a = np.empty((k // 512, 16))
    for p in range(k // 512):
        a[p, :8] = np.random.permutation(np.resize(levels, 8))
        for g in range(8):
            far = levels[np.abs(levels - a[p, g]) >= 10]
            a[p, g + 8] = far[np.random.randint(len(far))]
    return np.exp2(a.ravel()).repeat(32)


def f64(x):
    return np.asarray(x).astype(np.float64)


def striped(idx):
    return np.tile(idx.reshape(-1, 16).T, (8, 1)).astype(np.uint16)


def unstriped(offs):
    return offs[:16].T.reshape(-1).astype(np.int64)


E2M1 = np.array([0.0, 0.5, 1.0, 1.5, 2.0, 3.0, 4.0, 6.0, -0.0, -0.5, -1.0, -1.5, -2.0, -3.0, -4.0, -6.0])


def pack_weight(w, fmt):
    k, n = w.shape
    w = f64(np.asarray(w, np.float32).astype(ml_dtypes.bfloat16)).reshape(k // 32, 32, n)
    amax = np.abs(w).max(1)
    if fmt == "e4m3":
        byte = np.frexp(amax)[1] - 1 + 127 - 7
    else:
        mant, ex = np.frexp(amax / 6.0)
        byte = np.where(mant > 0.5, ex, ex - 1) + 127
    byte = np.clip(np.where(amax > 0, byte, 1), 1, 254)
    scaled = (w * np.exp2(127.0 - byte)[:, None, :]).reshape(k, n).astype(np.float32)
    by_word = np.ascontiguousarray(scaled.reshape(k // 512, 128, 4, n).transpose(0, 1, 3, 2))
    if fmt == "e4m3":
        words = by_word.astype(ml_dtypes.float8_e4m3fn).view(np.uint8)
    else:
        c = by_word.astype(ml_dtypes.float4_e2m1fn).view(np.uint8) & 0xF
        words = (c[..., 0::2] | (c[..., 1::2] << 4)).reshape(k // 512, 128, 2 * n)
    return np.ascontiguousarray(words), np.ascontiguousarray(byte.astype(np.uint8).reshape(k // 512, 16, n))


def unpack_weight(words, scales, fmt):
    g, _, n = scales.shape
    words = np.ascontiguousarray(words).reshape(g, 128, n, -1)
    if fmt == "e4m3":
        vals = words.view(ml_dtypes.float8_e4m3fn).astype(np.float64)
    else:
        nib = np.empty((g, 128, n, 4), np.uint8)
        nib[..., 0::2] = words & 0xF
        nib[..., 1::2] = words >> 4
        vals = E2M1[nib]
    vals = vals * np.repeat(np.exp2(scales.astype(np.float64) - 127.0), 8, axis=1)[..., None]
    return vals.transpose(0, 1, 3, 2).reshape(g * 512, n)


def sigmoid(v):
    return 1.0 / (1.0 + np.exp(-np.maximum(v, -700.0)))


K, T, E, C, H, N = 1536, 768, 4, 128, 512, 512


def by_expert(wq, xq):
    return np.concatenate([wq[e].T @ xq[:, e * C:(e + 1) * C] for e in range(E)], axis=1)


def setup_inputs():
    n = np.random.standard_normal
    s = mx_kscale(K)[:, None]
    u = mx_kscale(H)
    x = pack_weight(n((K, T)) * s, "e4m3")
    return {
        "x_words": x[0],
        "x_scales": x[1],
        "xr": n((N, T)).astype(np.float32),
        "w1": (n((E, K, H)) / np.sqrt(K) / s[None]).astype(np.float32),
        "w3": (n((E, K, H)) / np.sqrt(K) / s[None] * u[None, None, :]).astype(np.float32),
        "w2": (n((E, H, N)) / np.sqrt(H) / u[None, :, None]).astype(np.float32),
        "gate": np.tile(np.random.uniform(0.2, 1.0, E * C), (N, 1)).astype(np.float32),
        "offs": striped(np.random.permutation(T)[:E * C]),
    }


def reference(x_words, x_scales, xr, w1, w3, w2, gate, offs):
    idx = unstriped(offs)
    xq = unpack_weight(x_words, x_scales, "e4m3")[:, idx]
    h = sigmoid(by_expert(mxq(f64(w1), 1, "e4m3"), xq))
    h = h * by_expert(mxq(f64(w3), 1, "e4m3"), xq)
    y = by_expert(mxq(f64(w2), 1, "e4m3"), mxq(h, 0, "e4m3"))
    out = f64(xr).copy()
    out[:, idx] += f64(gate) * y
    return out

@@ -1,0 +1,214 @@
+from contextlib import ExitStack
+
+import concourse.mybir as mybir
+from concourse.masks import make_identity
+
+K, T, E, C, H, N = 1536, 768, 4, 128, 512, 512
+SLOTS = E * C
+FLOPS = 2 * SLOTS * (2 * K * H + H * N)
+
+F32 = mybir.dt.float32
+BF16 = mybir.dt.bfloat16
+I32 = mybir.dt.int32
+U32 = mybir.dt.uint32
+U16 = mybir.dt.uint16
+U8 = mybir.dt.uint8
+FP8X4 = mybir.dt.float8_e4m3fn_x4
+MULT = mybir.AluOpType.mult
+ADD = mybir.AluOpType.add
+SIGMOID = mybir.ActivationFunctionType.Sigmoid
+
+P = 128
+PACK = 4
+K_PASS = P * PACK
+PASSES = K // K_PASS
+ROW_BLOCKS = N // P
+OFFS_PER_COL = 16
+SCALAR_COLS_LAST = 160
+CAST_SLOTS = 5
+
+
+def tile_moe_res_glu_sigmoid_kernel(
+    tc, x_words, x_scales, xr, w1, w3, w2, gate, offs, out
+):
+    nc = tc.nc
+    with ExitStack() as ctx:
+        keep = ctx.enter_context(tc.tile_pool(name="keep", bufs=1))
+        raw_pool = ctx.enter_context(tc.tile_pool(name="raw", bufs=8))
+        code_pool = ctx.enter_context(tc.tile_pool(name="code", bufs=14))
+        work = ctx.enter_context(tc.tile_pool(name="work", bufs=2))
+        psum = ctx.enter_context(tc.psum_pool(name="psum", bufs=2))
+
+        cast_slots = [
+            keep.tile([P, PACK * H], BF16, name="cast_slot%d" % i, align_bytes=64) for i in range(CAST_SLOTS)
+        ]
+        used = [0]
+
+        def load_rows(rows):
+            width = rows.shape[1]
+            raw = raw_pool.tile([P, PACK, width], F32, name="raw", tag="raw", align_bytes=64)
+            nc.sync.dma_start(out=raw[:], in_=rows.rearrange("(p j) w -> p j w", j=PACK))
+            return raw
+
+        def quantize_rows(raw, scalar_cols):
+            width = raw.shape[2]
+            if scalar_cols == width:
+                used[0] = used[0] + 1
+            slot = cast_slots[used[0] % CAST_SLOTS][:, 0 : PACK * width]
+            grouped = slot.rearrange("p (w j) -> p w j", j=PACK)
+            for copy, cols in (
+                (nc.scalar.copy, slice(0, scalar_cols)),
+                (nc.vector.tensor_copy, slice(scalar_cols, width)),
+            ):
+                if cols.stop > cols.start:
+                    copy(
+                        grouped[:, cols, :].rearrange("p (c i) j -> p c j i", i=4),
+                        raw[:, :, cols].rearrange("p j (c i) -> p c j i", i=4),
+                    )
+            codes = code_pool.tile([P, width], U32, name="codes", align_bytes=64)
+            scales = code_pool.tile([P, width], U8, name="scales", align_bytes=64)
+            nc.vector.quantize_mx(out=codes[:].bitcast(FP8X4), scales=scales[:], in_=slot)
+            return codes, scales
+
+        token_scales = keep.tile([P, T], U8, name="token_scales", align_bytes=64)
+        nc.vector.memset(token_scales[:].bitcast(I32), 0)
+
+        offsets = keep.tile([P, SLOTS // OFFS_PER_COL], U16, name="offsets")
+        nc.sync.dma_start(offsets[:], offs)
+        token_words = []
+        for o in range(PASSES):
+            words = keep.tile([P, T], I32, name="token_words%d" % o, align_bytes=64)
+            nc.sync.dma_start(out=words[:], in_=x_words[o].rearrange("p t r -> p (t r)").bitcast(I32))
+            token_words.append(words)
+        first_raw = [load_rows(w1[0, o * K_PASS : (o + 1) * K_PASS, :]) for o in range(2)]
+        for q in range(4):
+            nc.sync.dma_start(
+                out=token_scales[32 * q : 32 * q + 4 * PASSES, :].bitcast(I32),
+                in_=x_scales[:, 4 * q : 4 * q + 4, :].bitcast(I32),
+            )
+        gate_rows = keep.tile([P, SLOTS], F32, name="gate_rows")
+        nc.sync.dma_start(out=gate_rows[:], in_=gate[0:P, :])
+
+        identity = keep.tile([P, P], F32, name="identity")
+        make_identity(nc, identity[:])
+        windows = []
+        for nb in range(ROW_BLOCKS):
+            window = keep.tile([P, T], F32, name="window%d" % nb)
+            nc.vector.memset(window[:], 0.0)
+            windows.append(window)
+
+        slot_words = []
+        for o in range(PASSES):
+            words = keep.tile([P, SLOTS], U32, name="slot_words%d" % o, align_bytes=64)
+            nc.vector.tensor_copy(words[:], token_words[o][:].bitcast(U32).indirect(offsets[:]))
+            slot_words.append(words)
+        slot_scales = keep.tile([P, SLOTS], U8, name="slot_scales", align_bytes=64)
+        nc.vector.tensor_copy(slot_scales[:], token_scales[:].indirect(offsets[:]))
+
+        def first_layer_pass(e, o, raw, acc, scalar_cols):
+            slots = slice(e * C, (e + 1) * C)
+            codes, scales = quantize_rows(raw, scalar_cols)
+            nc.tensor.matmul_mx(
+                out=acc[:],
+                lhsT=slot_words[o][:, slots].bitcast(FP8X4),
+                lhsT_scale=slot_scales[4 * o : P, slots],
+                rhs=codes[:].bitcast(FP8X4),
+                rhs_scale=scales[:],
+                start=(o == 0),
+                stop=(o == PASSES - 1),
+            )
+
+        def turn_hidden(b, sig):
+            h = work.tile([P, H], BF16, name="h", align_bytes=64)
+            nc.vector.tensor_tensor(h[:], b[:], sig, MULT)
+            h_words = h[:].bitcast(F32)
+            turned = psum.tile([P, 2, C], F32, name="turned", tag="turned")
+            for u in range(2):
+                nc.tensor.transpose(turned[:, u, :], h_words[:, u : H // 2 : 2], identity[:])
+            return turned
+
+        def second_layer(turned, spent, w2_parts):
+            h_pairs = spent[:, 0, 0 : 2 * C]
+            nc.scalar.copy(h_pairs.rearrange("p (s u) -> p s u", u=2), turned[:].rearrange("p u s -> p s u"))
+            h_codes = work.tile([P, C], U32, name="h_codes", align_bytes=64)
+            h_scales = work.tile([P, C], U8, name="h_scales", align_bytes=64)
+            nc.vector.quantize_mx(out=h_codes[:].bitcast(FP8X4), scales=h_scales[:], in_=h_pairs.bitcast(BF16))
+            banks = []
+            for w2_codes, w2_scales in w2_parts:
+                blocks = w2_codes.shape[1] // P
+                y = psum.tile([P, blocks * C], F32, name="y", tag="y")
+                for i in range(blocks):
+                    cols = slice(i * P, (i + 1) * P)
+                    nc.tensor.matmul_mx(
+                        out=y[:, i * C : (i + 1) * C],
+                        lhsT=w2_codes[:, cols].bitcast(FP8X4),
+                        lhsT_scale=w2_scales[:, cols],
+                        rhs=h_codes[:].bitcast(FP8X4),
+                        rhs_scale=h_scales[:],
+                        start=True,
+                        stop=True,
+                    )
+                banks.append(y)
+            return banks
+
+        def leave_psum(banks, y_sb):
+            at = 0
+            for y in banks:
+                nc.scalar.copy(y_sb[:, at : at + y.shape[1]], y[:])
+                at = at + y.shape[1]
+
+        def scatter(e, nb, y_sb):
+            cols_per_expert = C // OFFS_PER_COL
+            expert_offsets = offsets[:, e * cols_per_expert : (e + 1) * cols_per_expert]
+            nc.vector.tensor_tensor(
+                windows[nb][:].indirect(expert_offsets),
+                y_sb[:, nb * C : (nb + 1) * C],
+                gate_rows[:, e * C : (e + 1) * C],
+                MULT,
+            )
+
+        banks = None
+        for e in range(E):
+            last = e == E - 1
+            a = psum.tile([P, H], F32, name="a", tag="a")
+            for o in range(PASSES):
+                if e == 0 and o < len(first_raw):
+                    raw = first_raw[o]
+                else:
+                    raw = load_rows(w1[e, o * K_PASS : (o + 1) * K_PASS, :])
+                first_layer_pass(e, o, raw, a, 0 if o == 1 else H)
+                if e > 0 and o == 0:
+                    leave_psum(banks, raw[:, 0, :])
+                    for nb in range(ROW_BLOCKS):
+                        scatter(e - 1, nb, raw[:, 0, :])
+            b = psum.tile([P, H], F32, name="b", tag="b")
+            for o in range(PASSES):
+                raw = load_rows(w3[e, o * K_PASS : (o + 1) * K_PASS, :])
+                scalar_cols = 0 if o == 1 else H
+                if last and o == PASSES - 1:
+                    scalar_cols = SCALAR_COLS_LAST
+                first_layer_pass(e, o, raw, b, scalar_cols)
+                if o == 0:
+                    sig = raw[:, 0, :]
+                    nc.scalar.activation(sig, a[:], SIGMOID)
+            turned = turn_hidden(b, sig)
+            pieces = 2 if last else 1
+            width = N // pieces
+            w2_raws = [load_rows(w2[e, :, i * width : (i + 1) * width]) for i in range(pieces)]
+            w2_parts = [quantize_rows(raw, width) for raw in w2_raws]
+            banks = second_layer(turned, w2_raws[-1], w2_parts)
+
+        y_last = keep.tile([P, ROW_BLOCKS * C], F32, name="y_last")
+        leave_psum(banks, y_last[:])
+        residuals = []
+        for nb in range(ROW_BLOCKS):
+            residual = raw_pool.tile([P, T], F32, name="residual", tag="raw", align_bytes=64)
+            nc.sync.dma_start(out=residual[:], in_=xr[nb * P : (nb + 1) * P, :])
+            residuals.append(residual)
+        for step in range(ROW_BLOCKS + 1):
+            if step < ROW_BLOCKS:
+                scatter(E - 1, step, y_last[:])
+            if step > 0:
+                nb = step - 1
+                nc.vector.tensor_tensor(residuals[nb][:], residuals[nb][:], windows[nb][:], ADD)
+                nc.sync.dma_start(out=out[nb * P : (nb + 1) * P, :], in_=residuals[nb][:])

@@ -24,8 +24,10 @@ K_PASS = P * PACK
 PASSES = K // K_PASS
 ROW_BLOCKS = N // P
 OFFS_PER_COL = 16
-SCALAR_COLS_LAST = 160
-CAST_SLOTS = 5
+BUSY, FREE, L0, L1, EARLY, SPLIT = 304, 288, 192, 80, 3, 1
+SCALAR_COLS = [BUSY, BUSY, BUSY, BUSY, FREE, FREE, FREE]
+SCALAR_COLS_LAST = [L0, L1]
+HALF = H // 2
 
 
 def tile_moe_res_glu_sigmoid_kernel(
@@ -35,14 +37,10 @@ def tile_moe_res_glu_sigmoid_kernel(
     with ExitStack() as ctx:
         keep = ctx.enter_context(tc.tile_pool(name="keep", bufs=1))
         raw_pool = ctx.enter_context(tc.tile_pool(name="raw", bufs=8))
+        cast_pool = ctx.enter_context(tc.tile_pool(name="cast", bufs=4))
         code_pool = ctx.enter_context(tc.tile_pool(name="code", bufs=14))
         work = ctx.enter_context(tc.tile_pool(name="work", bufs=2))
         psum = ctx.enter_context(tc.psum_pool(name="psum", bufs=2))
-
-        cast_slots = [
-            keep.tile([P, PACK * H], BF16, name="cast_slot%d" % i, align_bytes=64) for i in range(CAST_SLOTS)
-        ]
-        used = [0]
 
         def load_rows(rows):
             width = rows.shape[1]
@@ -52,10 +50,8 @@ def tile_moe_res_glu_sigmoid_kernel(
 
         def quantize_rows(raw, scalar_cols):
             width = raw.shape[2]
-            if scalar_cols == width:
-                used[0] = used[0] + 1
-            slot = cast_slots[used[0] % CAST_SLOTS][:, 0 : PACK * width]
-            grouped = slot.rearrange("p (w j) -> p w j", j=PACK)
+            slot = cast_pool.tile([P, PACK * width], BF16, name="slot", align_bytes=64)
+            grouped = slot[:].rearrange("p (w j) -> p w j", j=PACK)
             for copy, cols in (
                 (nc.scalar.copy, slice(0, scalar_cols)),
                 (nc.vector.tensor_copy, slice(scalar_cols, width)),
@@ -67,7 +63,7 @@ def tile_moe_res_glu_sigmoid_kernel(
                     )
             codes = code_pool.tile([P, width], U32, name="codes", align_bytes=64)
             scales = code_pool.tile([P, width], U8, name="scales", align_bytes=64)
-            nc.vector.quantize_mx(out=codes[:].bitcast(FP8X4), scales=scales[:], in_=slot)
+            nc.vector.quantize_mx(out=codes[:].bitcast(FP8X4), scales=scales[:], in_=slot[:])
             return codes, scales
 
         token_scales = keep.tile([P, T], U8, name="token_scales", align_bytes=64)
@@ -105,24 +101,29 @@ def tile_moe_res_glu_sigmoid_kernel(
         slot_scales = keep.tile([P, SLOTS], U8, name="slot_scales", align_bytes=64)
         nc.vector.tensor_copy(slot_scales[:], token_scales[:].indirect(offsets[:]))
 
-        def first_layer_pass(e, o, raw, acc, scalar_cols):
+        def first_layer_pass(e, o, codes, scales, acc):
             slots = slice(e * C, (e + 1) * C)
-            codes, scales = quantize_rows(raw, scalar_cols)
             nc.tensor.matmul_mx(
-                out=acc[:],
+                out=acc,
                 lhsT=slot_words[o][:, slots].bitcast(FP8X4),
                 lhsT_scale=slot_scales[4 * o : P, slots],
-                rhs=codes[:].bitcast(FP8X4),
-                rhs_scale=scales[:],
+                rhs=codes.bitcast(FP8X4),
+                rhs_scale=scales,
                 start=(o == 0),
                 stop=(o == PASSES - 1),
             )
 
-        def turn_hidden(b, sig):
+        def turn_hidden(b_banks, sig):
             h = work.tile([P, H], BF16, name="h", align_bytes=64)
-            nc.vector.tensor_tensor(h[:], b[:], sig, MULT)
+            if len(b_banks) == 1:
+                nc.vector.tensor_tensor(
+                    h[:].rearrange("p (r c) -> p r c", r=2), b_banks[0][:].rearrange("p (r c) -> p r c", r=2), sig, MULT
+                )
+            else:
+                for r in range(2):
+                    nc.vector.tensor_tensor(h[:, r * HALF : (r + 1) * HALF], b_banks[r][:], sig[:, r, :], MULT)
             h_words = h[:].bitcast(F32)
-            turned = psum.tile([P, 2, C], F32, name="turned", tag="turned")
+            turned = psum.tile([P, 2, C], F32, name="turned", tag="turned", bufs=1)
             for u in range(2):
                 nc.tensor.transpose(turned[:, u, :], h_words[:, u : H // 2 : 2], identity[:])
             return turned
@@ -136,7 +137,7 @@ def tile_moe_res_glu_sigmoid_kernel(
             banks = []
             for w2_codes, w2_scales in w2_parts:
                 blocks = w2_codes.shape[1] // P
-                y = psum.tile([P, blocks * C], F32, name="y", tag="y")
+                y = psum.tile([P, blocks * C], F32, name="y", tag="y", bufs=3)
                 for i in range(blocks):
                     cols = slice(i * P, (i + 1) * P)
                     nc.tensor.matmul_mx(
@@ -157,12 +158,12 @@ def tile_moe_res_glu_sigmoid_kernel(
                 nc.scalar.copy(y_sb[:, at : at + y.shape[1]], y[:])
                 at = at + y.shape[1]
 
-        def scatter(e, nb, y_sb):
+        def scatter(e, nb, y_block):
             cols_per_expert = C // OFFS_PER_COL
             expert_offsets = offsets[:, e * cols_per_expert : (e + 1) * cols_per_expert]
             nc.vector.tensor_tensor(
                 windows[nb][:].indirect(expert_offsets),
-                y_sb[:, nb * C : (nb + 1) * C],
+                y_block,
                 gate_rows[:, e * C : (e + 1) * C],
                 MULT,
             )
@@ -171,33 +172,47 @@ def tile_moe_res_glu_sigmoid_kernel(
         for e in range(E):
             last = e == E - 1
             a = psum.tile([P, H], F32, name="a", tag="a")
-            for o in range(PASSES):
-                if e == 0 and o < len(first_raw):
-                    raw = first_raw[o]
+            b_width = HALF if last else H
+            b_banks = [psum.tile([P, b_width], F32, name="b", tag="b") for i in range(H // b_width)]
+            for step in range(2 * PASSES):
+                o = step % PASSES
+                rows = slice(o * K_PASS, (o + 1) * K_PASS)
+                if last and step == 2 * PASSES - 1:
+                    for r in range(2):
+                        half = load_rows(w3[e, rows, r * HALF : (r + 1) * HALF])
+                        codes, scales = quantize_rows(half, SCALAR_COLS_LAST[r])
+                        first_layer_pass(e, o, codes[:], scales[:], b_banks[r][:])
+                    continue
+                if e == 0 and step < len(first_raw):
+                    raw = first_raw[step]
                 else:
-                    raw = load_rows(w1[e, o * K_PASS : (o + 1) * K_PASS, :])
-                first_layer_pass(e, o, raw, a, 0 if o == 1 else H)
-                if e > 0 and o == 0:
-                    leave_psum(banks, raw[:, 0, :])
-                    for nb in range(ROW_BLOCKS):
-                        scatter(e - 1, nb, raw[:, 0, :])
-            b = psum.tile([P, H], F32, name="b", tag="b")
-            for o in range(PASSES):
-                raw = load_rows(w3[e, o * K_PASS : (o + 1) * K_PASS, :])
-                scalar_cols = 0 if o == 1 else H
-                if last and o == PASSES - 1:
-                    scalar_cols = SCALAR_COLS_LAST
-                first_layer_pass(e, o, raw, b, scalar_cols)
-                if o == 0:
-                    sig = raw[:, 0, :]
-                    nc.scalar.activation(sig, a[:], SIGMOID)
-            turned = turn_hidden(b, sig)
+                    raw = load_rows((w1 if step < PASSES else w3)[e, rows, :])
+                codes, scales = quantize_rows(raw, SCALAR_COLS[step])
+                if step < PASSES:
+                    first_layer_pass(e, o, codes[:], scales[:], a[:])
+                else:
+                    for r in range(len(b_banks)):
+                        cols = slice(r * b_width, (r + 1) * b_width)
+                        first_layer_pass(e, o, codes[:, cols], scales[:, cols], b_banks[r][:])
+                if e > 0 and step < (EARLY if last else ROW_BLOCKS):
+                    y_block = raw[:, 2, 0:C]
+                    nc.scalar.copy(y_block, banks[0][:, step * C : (step + 1) * C])
+                    scatter(e - 1, step, y_block)
+                if step == PASSES:
+                    sig = raw[:, 0:2, 0:HALF]
+                    nc.scalar.activation(sig, a[:].rearrange("p (r c) -> p r c", r=2), SIGMOID)
+            turned = turn_hidden(b_banks, sig)
             pieces = 2 if last else 1
             width = N // pieces
             w2_raws = [load_rows(w2[e, :, i * width : (i + 1) * width]) for i in range(pieces)]
-            w2_parts = [quantize_rows(raw, width) for raw in w2_raws]
+            w2_parts = [quantize_rows(raw, width if last else SCALAR_COLS[-1]) for raw in w2_raws]
+            earlier = banks
             banks = second_layer(turned, w2_raws[-1], w2_parts)
 
+        for nb in range(EARLY, ROW_BLOCKS):
+            y_block = w2_raws[-1][:, 2, 0:C]
+            nc.scalar.copy(y_block, earlier[0][:, nb * C : (nb + 1) * C])
+            scatter(E - 2, nb, y_block)
         y_last = keep.tile([P, ROW_BLOCKS * C], F32, name="y_last")
         leave_psum(banks, y_last[:])
         residuals = []
@@ -207,8 +222,11 @@ def tile_moe_res_glu_sigmoid_kernel(
             residuals.append(residual)
         for step in range(ROW_BLOCKS + 1):
             if step < ROW_BLOCKS:
-                scatter(E - 1, step, y_last[:])
+                scatter(E - 1, step, y_last[:, step * C : (step + 1) * C])
             if step > 0:
                 nb = step - 1
-                nc.vector.tensor_tensor(residuals[nb][:], residuals[nb][:], windows[nb][:], ADD)
-                nc.sync.dma_start(out=out[nb * P : (nb + 1) * P, :], in_=residuals[nb][:])
+                cuts = SPLIT if nb == ROW_BLOCKS - 1 else 1
+                for i in range(cuts):
+                    cols = slice(i * T // cuts, (i + 1) * T // cuts)
+                    nc.vector.tensor_tensor(residuals[nb][:, cols], residuals[nb][:, cols], windows[nb][:, cols], ADD)
+                    nc.sync.dma_start(out=out[nb * P : (nb + 1) * P, cols], in_=residuals[nb][:, cols])

@@ -24,8 +24,8 @@ K_PASS = P * PACK
 PASSES = K // K_PASS
 ROW_BLOCKS = N // P
 OFFS_PER_COL = 16
-BUSY, FREE, L0, L1, EARLY, SPLIT = 304, 288, 192, 80, 3, 1
-SCALAR_COLS = [BUSY, BUSY, BUSY, BUSY, FREE, FREE, FREE]
+BUSY, FREE, L0, L1, EARLY, SPLIT, L3, L4, SIGSTEP, W2S, HH = [256,256,256,256,256,256,256],[1,2,3,4],192,80,3,1,[256,256,256,256,256],0,3,[256,128],1
+SCALAR_COLS = BUSY
 SCALAR_COLS_LAST = [L0, L1]
 HALF = H // 2
 
@@ -58,8 +58,8 @@ def tile_moe_res_glu_sigmoid_kernel(
             ):
                 if cols.stop > cols.start:
                     copy(
-                        grouped[:, cols, :].rearrange("p (c i) j -> p c j i", i=4),
-                        raw[:, :, cols].rearrange("p j (c i) -> p c j i", i=4),
+                        grouped[:, cols, :].rearrange("p (c i) j -> p c j i", i=2),
+                        raw[:, :, cols].rearrange("p j (c i) -> p c j i", i=2),
                     )
             codes = code_pool.tile([P, width], U32, name="codes", align_bytes=64)
             scales = code_pool.tile([P, width], U8, name="scales", align_bytes=64)
@@ -113,23 +113,21 @@ def tile_moe_res_glu_sigmoid_kernel(
                 stop=(o == PASSES - 1),
             )
 
-        def turn_hidden(b_banks, sig):
-            h = work.tile([P, H], BF16, name="h", align_bytes=64)
+        def turn_hidden(b_banks, sig, h):
             if len(b_banks) == 1:
                 nc.vector.tensor_tensor(
-                    h[:].rearrange("p (r c) -> p r c", r=2), b_banks[0][:].rearrange("p (r c) -> p r c", r=2), sig, MULT
+                    h.rearrange("p (r c) -> p r c", r=2), b_banks[0][:].rearrange("p (r c) -> p r c", r=2), sig, MULT
                 )
             else:
                 for r in range(2):
                     nc.vector.tensor_tensor(h[:, r * HALF : (r + 1) * HALF], b_banks[r][:], sig[:, r, :], MULT)
-            h_words = h[:].bitcast(F32)
+            h_words = h.bitcast(F32)
             turned = psum.tile([P, 2, C], F32, name="turned", tag="turned", bufs=1)
             for u in range(2):
                 nc.tensor.transpose(turned[:, u, :], h_words[:, u : H // 2 : 2], identity[:])
             return turned
 
-        def second_layer(turned, spent, w2_parts):
-            h_pairs = spent[:, 0, 0 : 2 * C]
+        def second_layer(turned, h_pairs, w2_parts):
             nc.scalar.copy(h_pairs.rearrange("p (s u) -> p s u", u=2), turned[:].rearrange("p u s -> p s u"))
             h_codes = work.tile([P, C], U32, name="h_codes", align_bytes=64)
             h_scales = work.tile([P, C], U8, name="h_scales", align_bytes=64)
@@ -187,30 +185,37 @@ def tile_moe_res_glu_sigmoid_kernel(
                     raw = first_raw[step]
                 else:
                     raw = load_rows((w1 if step < PASSES else w3)[e, rows, :])
-                codes, scales = quantize_rows(raw, SCALAR_COLS[step])
+                codes, scales = quantize_rows(raw, L3[step] if last else SCALAR_COLS[step])
                 if step < PASSES:
                     first_layer_pass(e, o, codes[:], scales[:], a[:])
                 else:
                     for r in range(len(b_banks)):
                         cols = slice(r * b_width, (r + 1) * b_width)
                         first_layer_pass(e, o, codes[:, cols], scales[:, cols], b_banks[r][:])
-                if e > 0 and step < (EARLY if last else ROW_BLOCKS):
-                    y_block = raw[:, 2, 0:C]
-                    nc.scalar.copy(y_block, banks[0][:, step * C : (step + 1) * C])
-                    scatter(e - 1, step, y_block)
-                if step == PASSES:
+                if step == SIGSTEP:
                     sig = raw[:, 0:2, 0:HALF]
                     nc.scalar.activation(sig, a[:].rearrange("p (r c) -> p r c", r=2), SIGMOID)
-            turned = turn_hidden(b_banks, sig)
-            pieces = 2 if last else 1
-            width = N // pieces
-            w2_raws = [load_rows(w2[e, :, i * width : (i + 1) * width]) for i in range(pieces)]
-            w2_parts = [quantize_rows(raw, width if last else SCALAR_COLS[-1]) for raw in w2_raws]
-            earlier = banks
-            banks = second_layer(turned, w2_raws[-1], w2_parts)
+                if e > 0 and step == 0:
+                    banks = second_layer(turned, raw[:, 0, 0 : 2 * C], w2_parts)
+                here = [nb for nb in range(EARLY if last else ROW_BLOCKS) if FREE[nb] == step]
+                if e > 0 and here:
+                    y_block = raw[:, 2, 0 : len(here) * C]
+                    nc.scalar.copy(y_block, banks[0][:, here[0] * C : (here[-1] + 1) * C])
+                    for i, nb in enumerate(here):
+                        scatter(e - 1, nb, y_block[:, i * C : (i + 1) * C])
+            if not last:
+                raw = load_rows(w2[e])
+                w2_parts = [quantize_rows(raw, SCALAR_COLS[-1])]
+                turned = turn_hidden(b_banks, sig, raw[:, 0, 0:HALF].bitcast(BF16))
 
+        h_last = keep.tile([P, H], BF16, name="h", align_bytes=64)
+        turned = turn_hidden(b_banks, sig, h_last[:])
+        w2_raws = [load_rows(w2[E - 1, :, i * HALF : (i + 1) * HALF]) for i in range(2)]
+        w2_parts = [quantize_rows(w2_raws[i], W2S[i]) for i in range(2)]
+        earlier = banks
+        banks = second_layer(turned, w2_raws[HH][:, 0, 0 : 2 * C], w2_parts)
         for nb in range(EARLY, ROW_BLOCKS):
-            y_block = w2_raws[-1][:, 2, 0:C]
+            y_block = w2_raws[HH][:, 2, 0:C]
             nc.scalar.copy(y_block, earlier[0][:, nb * C : (nb + 1) * C])
             scatter(E - 2, nb, y_block)
         y_last = keep.tile([P, ROW_BLOCKS * C], F32, name="y_last")

from contextlib import ExitStack

import concourse.mybir as mybir
from concourse.masks import make_identity

K, T, E, C, H, N = 1536, 768, 4, 128, 512, 512
SLOTS = E * C
FLOPS = 2 * SLOTS * (2 * K * H + H * N)

F32 = mybir.dt.float32
BF16 = mybir.dt.bfloat16
I32 = mybir.dt.int32
U32 = mybir.dt.uint32
U16 = mybir.dt.uint16
U8 = mybir.dt.uint8
FP8X4 = mybir.dt.float8_e4m3fn_x4
MULT = mybir.AluOpType.mult
ADD = mybir.AluOpType.add
SIGMOID = mybir.ActivationFunctionType.Sigmoid

P = 128
PACK = 4
K_PASS = P * PACK
PASSES = K // K_PASS
ROW_BLOCKS = N // P
OFFS_PER_COL = 16
BUSY, FREE, L0, L1, EARLY, SPLIT, L3, L4, SIGSTEP, W2S, HH = [256,256,256,256,256,256,256],[1,2,3,4],192,80,3,1,[256,256,256,256,256],0,3,[256,128],1
SCALAR_COLS = BUSY
SCALAR_COLS_LAST = [L0, L1]
HALF = H // 2


def tile_moe_res_glu_sigmoid_kernel(
    tc, x_words, x_scales, xr, w1, w3, w2, gate, offs, out
):
    nc = tc.nc
    with ExitStack() as ctx:
        keep = ctx.enter_context(tc.tile_pool(name="keep", bufs=1))
        raw_pool = ctx.enter_context(tc.tile_pool(name="raw", bufs=8))
        cast_pool = ctx.enter_context(tc.tile_pool(name="cast", bufs=4))
        code_pool = ctx.enter_context(tc.tile_pool(name="code", bufs=14))
        work = ctx.enter_context(tc.tile_pool(name="work", bufs=2))
        psum = ctx.enter_context(tc.psum_pool(name="psum", bufs=2))

        def load_rows(rows):
            width = rows.shape[1]
            raw = raw_pool.tile([P, PACK, width], F32, name="raw", tag="raw", align_bytes=64)
            nc.sync.dma_start(out=raw[:], in_=rows.rearrange("(p j) w -> p j w", j=PACK))
            return raw

        def quantize_rows(raw, scalar_cols):
            width = raw.shape[2]
            slot = cast_pool.tile([P, PACK * width], BF16, name="slot", align_bytes=64)
            grouped = slot[:].rearrange("p (w j) -> p w j", j=PACK)
            for copy, cols in (
                (nc.scalar.copy, slice(0, scalar_cols)),
                (nc.vector.tensor_copy, slice(scalar_cols, width)),
            ):
                if cols.stop > cols.start:
                    copy(
                        grouped[:, cols, :].rearrange("p (c i) j -> p c j i", i=2),
                        raw[:, :, cols].rearrange("p j (c i) -> p c j i", i=2),
                    )
            codes = code_pool.tile([P, width], U32, name="codes", align_bytes=64)
            scales = code_pool.tile([P, width], U8, name="scales", align_bytes=64)
            nc.vector.quantize_mx(out=codes[:].bitcast(FP8X4), scales=scales[:], in_=slot[:])
            return codes, scales

        token_scales = keep.tile([P, T], U8, name="token_scales", align_bytes=64)
        nc.vector.memset(token_scales[:].bitcast(I32), 0)

        offsets = keep.tile([P, SLOTS // OFFS_PER_COL], U16, name="offsets")
        nc.sync.dma_start(offsets[:], offs)
        token_words = []
        for o in range(PASSES):
            words = keep.tile([P, T], I32, name="token_words%d" % o, align_bytes=64)
            nc.sync.dma_start(out=words[:], in_=x_words[o].rearrange("p t r -> p (t r)").bitcast(I32))
            token_words.append(words)
        first_raw = [load_rows(w1[0, o * K_PASS : (o + 1) * K_PASS, :]) for o in range(2)]
        for q in range(4):
            nc.sync.dma_start(
                out=token_scales[32 * q : 32 * q + 4 * PASSES, :].bitcast(I32),
                in_=x_scales[:, 4 * q : 4 * q + 4, :].bitcast(I32),
            )
        gate_rows = keep.tile([P, SLOTS], F32, name="gate_rows")
        nc.sync.dma_start(out=gate_rows[:], in_=gate[0:P, :])

        identity = keep.tile([P, P], F32, name="identity")
        make_identity(nc, identity[:])
        windows = []
        for nb in range(ROW_BLOCKS):
            window = keep.tile([P, T], F32, name="window%d" % nb)
            nc.vector.memset(window[:], 0.0)
            windows.append(window)

        slot_words = []
        for o in range(PASSES):
            words = keep.tile([P, SLOTS], U32, name="slot_words%d" % o, align_bytes=64)
            nc.vector.tensor_copy(words[:], token_words[o][:].bitcast(U32).indirect(offsets[:]))
            slot_words.append(words)
        slot_scales = keep.tile([P, SLOTS], U8, name="slot_scales", align_bytes=64)
        nc.vector.tensor_copy(slot_scales[:], token_scales[:].indirect(offsets[:]))

        def first_layer_pass(e, o, codes, scales, acc):
            slots = slice(e * C, (e + 1) * C)
            nc.tensor.matmul_mx(
                out=acc,
                lhsT=slot_words[o][:, slots].bitcast(FP8X4),
                lhsT_scale=slot_scales[4 * o : P, slots],
                rhs=codes.bitcast(FP8X4),
                rhs_scale=scales,
                start=(o == 0),
                stop=(o == PASSES - 1),
            )

        def turn_hidden(b_banks, sig, h):
            if len(b_banks) == 1:
                nc.vector.tensor_tensor(
                    h.rearrange("p (r c) -> p r c", r=2), b_banks[0][:].rearrange("p (r c) -> p r c", r=2), sig, MULT
                )
            else:
                for r in range(2):
                    nc.vector.tensor_tensor(h[:, r * HALF : (r + 1) * HALF], b_banks[r][:], sig[:, r, :], MULT)
            h_words = h.bitcast(F32)
            turned = psum.tile([P, 2, C], F32, name="turned", tag="turned", bufs=1)
            for u in range(2):
                nc.tensor.transpose(turned[:, u, :], h_words[:, u : H // 2 : 2], identity[:])
            return turned

        def second_layer(turned, h_pairs, w2_parts):
            nc.scalar.copy(h_pairs.rearrange("p (s u) -> p s u", u=2), turned[:].rearrange("p u s -> p s u"))
            h_codes = work.tile([P, C], U32, name="h_codes", align_bytes=64)
            h_scales = work.tile([P, C], U8, name="h_scales", align_bytes=64)
            nc.vector.quantize_mx(out=h_codes[:].bitcast(FP8X4), scales=h_scales[:], in_=h_pairs.bitcast(BF16))
            banks = []
            for w2_codes, w2_scales in w2_parts:
                blocks = w2_codes.shape[1] // P
                y = psum.tile([P, blocks * C], F32, name="y", tag="y", bufs=3)
                for i in range(blocks):
                    cols = slice(i * P, (i + 1) * P)
                    nc.tensor.matmul_mx(
                        out=y[:, i * C : (i + 1) * C],
                        lhsT=w2_codes[:, cols].bitcast(FP8X4),
                        lhsT_scale=w2_scales[:, cols],
                        rhs=h_codes[:].bitcast(FP8X4),
                        rhs_scale=h_scales[:],
                        start=True,
                        stop=True,
                    )
                banks.append(y)
            return banks

        def leave_psum(banks, y_sb):
            at = 0
            for y in banks:
                nc.scalar.copy(y_sb[:, at : at + y.shape[1]], y[:])
                at = at + y.shape[1]

        def scatter(e, nb, y_block):
            cols_per_expert = C // OFFS_PER_COL
            expert_offsets = offsets[:, e * cols_per_expert : (e + 1) * cols_per_expert]
            nc.vector.tensor_tensor(
                windows[nb][:].indirect(expert_offsets),
                y_block,
                gate_rows[:, e * C : (e + 1) * C],
                MULT,
            )

        banks = None
        for e in range(E):
            last = e == E - 1
            a = psum.tile([P, H], F32, name="a", tag="a")
            b_width = HALF if last else H
            b_banks = [psum.tile([P, b_width], F32, name="b", tag="b") for i in range(H // b_width)]
            for step in range(2 * PASSES):
                o = step % PASSES
                rows = slice(o * K_PASS, (o + 1) * K_PASS)
                if last and step == 2 * PASSES - 1:
                    for r in range(2):
                        half = load_rows(w3[e, rows, r * HALF : (r + 1) * HALF])
                        codes, scales = quantize_rows(half, SCALAR_COLS_LAST[r])
                        first_layer_pass(e, o, codes[:], scales[:], b_banks[r][:])
                    continue
                if e == 0 and step < len(first_raw):
                    raw = first_raw[step]
                else:
                    raw = load_rows((w1 if step < PASSES else w3)[e, rows, :])
                codes, scales = quantize_rows(raw, L3[step] if last else SCALAR_COLS[step])
                if step < PASSES:
                    first_layer_pass(e, o, codes[:], scales[:], a[:])
                else:
                    for r in range(len(b_banks)):
                        cols = slice(r * b_width, (r + 1) * b_width)
                        first_layer_pass(e, o, codes[:, cols], scales[:, cols], b_banks[r][:])
                if step == SIGSTEP:
                    sig = raw[:, 0:2, 0:HALF]
                    nc.scalar.activation(sig, a[:].rearrange("p (r c) -> p r c", r=2), SIGMOID)
                if e > 0 and step == 0:
                    banks = second_layer(turned, raw[:, 0, 0 : 2 * C], w2_parts)
                here = [nb for nb in range(EARLY if last else ROW_BLOCKS) if FREE[nb] == step]
                if e > 0 and here:
                    y_block = raw[:, 2, 0 : len(here) * C]
                    nc.scalar.copy(y_block, banks[0][:, here[0] * C : (here[-1] + 1) * C])
                    for i, nb in enumerate(here):
                        scatter(e - 1, nb, y_block[:, i * C : (i + 1) * C])
            if not last:
                raw = load_rows(w2[e])
                w2_parts = [quantize_rows(raw, SCALAR_COLS[-1])]
                turned = turn_hidden(b_banks, sig, raw[:, 0, 0:HALF].bitcast(BF16))

        h_last = keep.tile([P, H], BF16, name="h", align_bytes=64)
        turned = turn_hidden(b_banks, sig, h_last[:])
        w2_raws = [load_rows(w2[E - 1, :, i * HALF : (i + 1) * HALF]) for i in range(2)]
        w2_parts = [quantize_rows(w2_raws[i], W2S[i]) for i in range(2)]
        earlier = banks
        banks = second_layer(turned, w2_raws[HH][:, 0, 0 : 2 * C], w2_parts)
        for nb in range(EARLY, ROW_BLOCKS):
            y_block = w2_raws[HH][:, 2, 0:C]
            nc.scalar.copy(y_block, earlier[0][:, nb * C : (nb + 1) * C])
            scatter(E - 2, nb, y_block)
        y_last = keep.tile([P, ROW_BLOCKS * C], F32, name="y_last")
        leave_psum(banks, y_last[:])
        residuals = []
        for nb in range(ROW_BLOCKS):
            residual = raw_pool.tile([P, T], F32, name="residual", tag="raw", align_bytes=64)
            nc.sync.dma_start(out=residual[:], in_=xr[nb * P : (nb + 1) * P, :])
            residuals.append(residual)
        for step in range(ROW_BLOCKS + 1):
            if step < ROW_BLOCKS:
                scatter(E - 1, step, y_last[:, step * C : (step + 1) * C])
            if step > 0:
                nb = step - 1
                cuts = SPLIT if nb == ROW_BLOCKS - 1 else 1
                for i in range(cuts):
                    cols = slice(i * T // cuts, (i + 1) * T // cuts)
                    nc.vector.tensor_tensor(residuals[nb][:, cols], residuals[nb][:, cols], windows[nb][:, cols], ADD)
                    nc.sync.dma_start(out=out[nb * P : (nb + 1) * P, cols], in_=residuals[nb][:, cols])
